import numpy as np
import ml_dtypes


def mxq(x, axis, fmt="e4m3"):
    dtype, down = {"e4m3": (ml_dtypes.float8_e4m3fn, 7), "e5m2": (ml_dtypes.float8_e5m2, 14)}[fmt]
    v = np.moveaxis(np.asarray(x, np.float32).astype(ml_dtypes.bfloat16).astype(np.float64), axis, -1)
    blocks = v.reshape(v.shape[:-1] + (-1, 32))
    amax = np.abs(blocks).max(-1, keepdims=True)
    byte = np.maximum(np.where(amax > 0, np.frexp(amax)[1] - 1 + 127, 0) - down, 1)
    scale = np.exp2(byte - 127.0)
    codes = (blocks / scale).astype(np.float32).astype(dtype).astype(np.float64)
    return np.moveaxis((codes * scale).reshape(v.shape), -1, axis)


WIDE = False


def mx_kscale(k):
    if not WIDE:
        return np.ones(k)
    levels = np.array([10, -10, 5, -5, 0])
    if k % 512:
        return np.exp2(np.random.permutation(np.resize(levels, k // 32))).repeat(32)
    a = np.empty((k // 512, 16))
    for p in range(k // 512):
        a[p, :8] = np.random.permutation(np.resize(levels, 8))
        for g in range(8):
            far = levels[np.abs(levels - a[p, g]) >= 10]
            a[p, g + 8] = far[np.random.randint(len(far))]
    return np.exp2(a.ravel()).repeat(32)


def f64(x):
    return np.asarray(x).astype(np.float64)


def striped(idx):
    return np.tile(np.asarray(idx).reshape(-1, 16).T, (8, 1)).astype(np.uint16)


def unstriped(offs):
    return offs[:16].T.reshape(-1).astype(np.int64)


E2M1 = np.array([0.0, 0.5, 1.0, 1.5, 2.0, 3.0, 4.0, 6.0, -0.0, -0.5, -1.0, -1.5, -2.0, -3.0, -4.0, -6.0])


def pack_weight(w, fmt):
    k, n = w.shape
    w = f64(np.asarray(w, np.float32).astype(ml_dtypes.bfloat16)).reshape(k // 32, 32, n)
    amax = np.abs(w).max(1)
    if fmt == "e4m3":
        byte = np.frexp(amax)[1] - 1 + 127 - 7
    else:
        mant, ex = np.frexp(amax / 6.0)
        byte = np.where(mant > 0.5, ex, ex - 1) + 127
    byte = np.clip(np.where(amax > 0, byte, 1), 1, 254)
    scaled = (w * np.exp2(127.0 - byte)[:, None, :]).reshape(k, n).astype(np.float32)
    by_word = np.ascontiguousarray(scaled.reshape(k // 512, 128, 4, n).transpose(0, 1, 3, 2))
    if fmt == "e4m3":
        words = by_word.astype(ml_dtypes.float8_e4m3fn).view(np.uint8)
    else:
        c = by_word.astype(ml_dtypes.float4_e2m1fn).view(np.uint8) & 0xF
        words = (c[..., 0::2] | (c[..., 1::2] << 4)).reshape(k // 512, 128, 2 * n)
    return np.ascontiguousarray(words), np.ascontiguousarray(byte.astype(np.uint8).reshape(k // 512, 16, n))


def unpack_weight(words, scales, fmt):
    g, _, n = scales.shape
    words = np.ascontiguousarray(words).reshape(g, 128, n, -1)
    if fmt == "e4m3":
        vals = words.view(ml_dtypes.float8_e4m3fn).astype(np.float64)
    else:
        nib = np.empty((g, 128, n, 4), np.uint8)
        nib[..., 0::2] = words & 0xF
        nib[..., 1::2] = words >> 4
        vals = E2M1[nib]
    vals = vals * np.repeat(np.exp2(scales.astype(np.float64) - 127.0), 8, axis=1)[..., None]
    return vals.transpose(0, 1, 3, 2).reshape(g * 512, n)


D, T, I, Q, J, G, M = 512, 2048, 512, 128, 512, 64, 512


def setup_inputs():
    n = np.random.standard_normal
    idx = np.random.permutation(T)[:I]
    idx2 = np.random.permutation(T)[:J]
    idx3 = np.random.permutation(M)[:G]
    fd = mx_kscale(D)
    fj = mx_kscale(J)
    keysp = pack_weight(n((D, T)) / fd[:, None], "e2m1")
    return {
        "query": (n((D, Q)) * 0.6 / np.sqrt(D) * fd[:, None]).astype(np.float32),
        "keys_words": keysp[0],
        "keys_scales": keysp[1],
        "hf": (np.random.uniform(0.5, 2.0, (J, 1)) * fj[:, None]).astype(np.float32),
        "mixer": (n((J, I)) * 0.05 / fj[:, None]).astype(np.float32),
        "lean": (np.random.uniform(0.2, 0.6, (Q, 1))).astype(np.float32),
        "worth": np.tile(np.random.uniform(0.2, 2.0, T), (128, 1)).astype(np.float32),
        "old": (1.0 * n((Q, M))).astype(np.float32),
        "offs": striped(idx),
        "offs2": striped(idx2),
        "offs3": striped(idx3),
    }


def reference(query, keys_words, keys_scales, hf, mixer, lean, worth, old, offs, offs2, offs3):
    idx = unstriped(offs)
    idx2 = unstriped(offs2)
    idx3 = unstriped(offs3)
    keysu = unpack_weight(keys_words, keys_scales, "e2m1")
    keysidx2g = keysu[:, idx2]
    queryq = mxq(f64(query), 0, "e4m3")
    a0 = keysidx2g.T @ queryq
    af = a0 * f64(hf)
    afq = mxq(af, 0, "e4m3")
    mixerq = mxq(f64(mixer), 0, "e4m3")
    mx0 = afq.T @ mixerq
    keysidxg = keysu[:, idx]
    a = queryq.T @ keysidxg
    s = a + mx0
    p = np.exp(s - np.max(s, axis=1, keepdims=True))
    r = p / np.sum(p, axis=1, keepdims=True)
    m0 = np.sum(r * s, axis=1, keepdims=True)
    w = r * ((s - m0) * f64(lean) + 1.0)
    ws = w * f64(worth)[:1][:, idx] * 256.0
    wp = ws.reshape(Q, G, I // G).sum(axis=2)
    wf = np.zeros((Q, M))
    wf[:, idx3] = wp
    y = f64(old) + wf
    return y

@@ -1,0 +1,186 @@
+from contextlib import ExitStack
+
+import concourse.mybir as mybir
+from concourse.masks import make_identity
+
+F32 = mybir.dt.float32
+BF16 = mybir.dt.bfloat16
+I32 = mybir.dt.int32
+U32 = mybir.dt.uint32
+U16 = mybir.dt.uint16
+U8 = mybir.dt.uint8
+FP8X4 = mybir.dt.float8_e4m3fn_x4
+FP4X4 = mybir.dt.float4_e2m1fn_x4
+ALU = mybir.AluOpType
+ACT = mybir.ActivationFunctionType
+AXIS = mybir.AxisListType
+
+P = 128
+PACK = 4
+D, T, I, Q, J, G, M = 512, 2048, 512, 128, 512, 64, 512
+RUN = I // G
+HALF = I // 2
+GAIN = 256.0
+
+FLOPS = 3 * 2 * 512 * 128 * 512
+
+
+def interleave(nc, dst, src):
+    nc.scalar.copy(
+        out=dst.rearrange("p (c i) t -> p c t i", i=4),
+        in_=src.rearrange("p t (c i) -> p c t i", i=4),
+    )
+
+
+def tile_attend_mixedslots_leaning_pagesums_kernel(
+    tc, query, keys_words, keys_scales, hf, mixer, lean, worth, old, offs, offs2, offs3, out
+):
+    nc = tc.nc
+    with ExitStack() as ctx:
+        sb = ctx.enter_context(tc.tile_pool(name="sb", bufs=1))
+        ps = ctx.enter_context(tc.psum_pool(name="ps", bufs=1))
+
+        key_scales = sb.tile([P, T], U8, align_bytes=64)
+        nc.vector.memset(key_scales[:].bitcast(I32), 0)
+
+        list2 = sb.tile([P, J // 16], U16)
+        nc.sync.dma_start(list2[:], offs2)
+        for quad in range(4):
+            nc.sync.dma_start(
+                key_scales[32 * quad : 32 * quad + 4, :].bitcast(I32),
+                keys_scales[0, 4 * quad : 4 * quad + 4, :].bitcast(I32),
+            )
+        key_words = sb.tile([P, T], U16, align_bytes=64)
+        nc.sync.dma_start(key_words[:].bitcast(I32), keys_words[0].bitcast(I32))
+        query_raw = sb.tile([P, PACK, Q], F32)
+        nc.sync.dma_start(query_raw[:], query.rearrange("(p t) q -> p t q", t=PACK))
+        mixer_rows = mixer.rearrange("(p t) i -> p t i", t=PACK)
+        mixer_raw = [sb.tile([P, PACK, HALF], F32, name=f"mixer_raw{h}") for h in range(2)]
+        nc.sync.dma_start(mixer_raw[0][:], mixer_rows[:, :, 0:HALF])
+        list1 = sb.tile([P, I // 16], U16)
+        nc.sync.dma_start(list1[:], offs)
+        nc.sync.dma_start(mixer_raw[1][:], mixer_rows[:, :, HALF:I])
+        worth_all = sb.tile([P, T], F32)
+        nc.sync.dma_start(worth_all[:], worth)
+        old_sb = sb.tile([P, M], F32)
+        nc.sync.dma_start(old_sb[:], old)
+        list3 = sb.tile([P, G // 16], U16)
+        nc.sync.dma_start(list3[:], offs3)
+
+        identity = sb.tile([P, P], F32)
+        make_identity(nc, identity[:])
+        hf_sb = sb.tile([P, PACK], F32)
+        nc.gpsimd.dma_start(hf_sb[:], hf.rearrange("(p t) o -> p (t o)", t=PACK))
+        lean_sb = sb.tile([P, 1], F32)
+        nc.gpsimd.dma_start(lean_sb[:], lean)
+        placed = sb.tile([P, M], F32)
+        nc.vector.memset(placed[:], 0.0)
+        lean_neg = sb.tile([P, 1], F32)
+        nc.gpsimd.tensor_scalar(lean_neg[:], lean_sb[:], -GAIN, 0.0, ALU.mult, ALU.add)
+
+        warm = sb.tile([P, 1], F32)
+        nc.scalar.activation(warm[:], placed[:, 0:1], ACT.Exp)
+
+        scales2 = sb.tile([P, J], U8, align_bytes=64)
+        nc.vector.tensor_copy(scales2[:], key_scales[:].indirect(list2[:]))
+        words2 = sb.tile([P, J], U16, align_bytes=64)
+        nc.vector.tensor_copy(words2[:], key_words[:].indirect(list2[:]))
+
+        query_bf = sb.tile([P, Q, PACK], BF16, align_bytes=64)
+        interleave(nc, query_bf[:], query_raw[:])
+        query_codes = sb.tile([P, Q], U32, align_bytes=64)
+        query_scales = sb.tile([P, Q], U8, align_bytes=64)
+        nc.vector.quantize_mx(
+            out=query_codes[:].bitcast(FP8X4), scales=query_scales[:], in_=query_bf[:].rearrange("p q t -> p (q t)")
+        )
+
+        a0_ps = ps.tile([P, J], F32)
+        nc.tensor.matmul_mx(
+            out=a0_ps[:], lhsT=query_codes[:].bitcast(FP8X4), lhsT_scale=query_scales[:],
+            rhs=words2[:].bitcast(FP4X4), rhs_scale=scales2[:], start=True, stop=True,
+        )
+
+        scales1 = sb.tile([P, I], U8, align_bytes=64)
+        nc.vector.tensor_copy(scales1[:], key_scales[:].indirect(list1[:]))
+        words1 = sb.tile([P, I], U16, align_bytes=64)
+        nc.vector.tensor_copy(words1[:], key_words[:].indirect(list1[:]))
+
+        mixer_codes = sb.tile([P, I], U32, align_bytes=64)
+        mixer_scales = sb.tile([P, I], U8, align_bytes=64)
+        mixer_bf = [sb.tile([P, HALF, PACK], BF16, align_bytes=64, name=f"mixer_bf{h}") for h in range(2)]
+        interleave(nc, mixer_bf[0][:], mixer_raw[0][:])
+
+        a0_sb = sb.tile([P, PACK, P], F32)
+        nc.scalar.copy(out=a0_sb[:], in_=a0_ps[:].rearrange("q (p t) -> q t p", t=PACK))
+        a0t_ps = ps.tile([P, PACK, Q], F32)
+        for t in range(PACK):
+            nc.tensor.transpose(a0t_ps[:, t, :], a0_sb[:, t, :], identity[:])
+
+        interleave(nc, mixer_bf[1][:], mixer_raw[1][:])
+
+        s_ps = ps.tile([P, I], F32)
+        nc.tensor.matmul_mx(
+            out=s_ps[:], lhsT=query_codes[:].bitcast(FP8X4), lhsT_scale=query_scales[:],
+            rhs=words1[:].bitcast(FP4X4), rhs_scale=scales1[:], start=True, stop=False,
+        )
+
+        af_bf = sb.tile([P, Q, PACK], BF16, align_bytes=64)
+        nc.vector.tensor_tensor(
+            af_bf[:], a0t_ps[:].rearrange("p t q -> p q t"),
+            hf_sb[:].unsqueeze(1).to_broadcast([P, Q, PACK]), ALU.mult,
+        )
+        for h in range(2):
+            cols = slice(h * HALF, (h + 1) * HALF)
+            nc.vector.quantize_mx(
+                out=mixer_codes[:, cols].bitcast(FP8X4), scales=mixer_scales[:, cols],
+                in_=mixer_bf[h][:].rearrange("p i t -> p (i t)"),
+            )
+        af_codes = sb.tile([P, Q], U32, align_bytes=64)
+        af_scales = sb.tile([P, Q], U8, align_bytes=64)
+        nc.vector.quantize_mx(
+            out=af_codes[:].bitcast(FP8X4), scales=af_scales[:], in_=af_bf[:].rearrange("p q t -> p (q t)")
+        )
+        nc.tensor.matmul_mx(
+            out=s_ps[:], lhsT=af_codes[:].bitcast(FP8X4), lhsT_scale=af_scales[:],
+            rhs=mixer_codes[:].bitcast(FP8X4), rhs_scale=mixer_scales[:], start=False, stop=True,
+        )
+
+        worth_slot = sb.tile([P, I], F32)
+        nc.vector.tensor_copy(worth_slot[:, 0:HALF], worth_all[:].indirect(list1[:, 0 : HALF // 16]))
+
+        s_neg = sb.tile([P, I], F32)
+        max_neg = sb.tile([P, 1], F32)
+        nc.vector.tensor_scalar(s_neg[:], s_ps[:], -1.0, None, ALU.mult, ALU.min, accum_out=max_neg[:])
+        p = sb.tile([P, I], F32)
+        p_sum = sb.tile([P, 1], F32)
+        nc.scalar.activation(p[:], s_ps[:], ACT.Exp, bias=max_neg[:], accum_out=p_sum[:])
+        tilt = sb.tile([P, I], F32)
+        nc.vector.tensor_scalar(tilt[:], s_neg[:], max_neg[:], lean_neg[:], ALU.subtract, ALU.mult)
+        nc.vector.tensor_copy(worth_slot[:, HALF:I], worth_all[:].indirect(list1[:, HALF // 16 : I // 16]))
+
+        p_inv = sb.tile([P, 1], F32)
+        nc.vector.reciprocal(p_inv[:], p_sum[:])
+        p_tilt = sb.tile([P, I], F32)
+        tilt_sum = sb.tile([P, 1], F32)
+        nc.vector.scalar_tensor_tensor(p_tilt[:], tilt[:], -GAIN, p[:], ALU.add, ALU.mult, accum_out=tilt_sum[:])
+        share = sb.tile([P, I], F32)
+        nc.vector.scalar_tensor_tensor(share[:], p[:], p_inv[:], worth_slot[:], ALU.mult, ALU.mult)
+        centre = sb.tile([P, 1], F32)
+        nc.vector.tensor_scalar(centre[:], tilt_sum[:], p_inv[:], None, ALU.mult)
+        ws = sb.tile([P, I], F32)
+        wp = sb.tile([P, G], F32)
+        for h in range(2):
+            cols = slice(h * HALF, (h + 1) * HALF)
+            nc.vector.scalar_tensor_tensor(ws[:, cols], tilt[:, cols], centre[:], share[:, cols], ALU.subtract, ALU.mult)
+        for h in range(2):
+            cols = slice(h * HALF, (h + 1) * HALF)
+            nc.vector.tensor_reduce(
+                wp[:, h * (G // 2) : (h + 1) * (G // 2)],
+                ws[:, cols].rearrange("q (g r) -> q g r", r=RUN), AXIS.X, ALU.add,
+            )
+        nc.vector.tensor_copy(placed[:].indirect(list3[:]), wp[:])
+        result = sb.tile([P, M], F32)
+        for h, queue in enumerate((nc.sync, nc.scalar)):
+            cols = slice(h * (M // 2), (h + 1) * (M // 2))
+            nc.vector.tensor_tensor(result[:, cols], placed[:, cols], old_sb[:, cols], ALU.add)
+            queue.dma_start(out[:, cols], result[:, cols])

@@ -21,6 +21,7 @@ D, T, I, Q, J, G, M = 512, 2048, 512, 128, 512, 64, 512
 RUN = I // G
 HALF = I // 2
 GAIN = 256.0
+CHUNKS = ((0, 256), (256, 512))
 
 FLOPS = 3 * 2 * 512 * 128 * 512
 
@@ -41,8 +42,10 @@ def tile_attend_mixedslots_leaning_pagesums_kernel(
         ps = ctx.enter_context(tc.psum_pool(name="ps", bufs=1))
 
         key_scales = sb.tile([P, T], U8, align_bytes=64)
-        nc.vector.memset(key_scales[:].bitcast(I32), 0)
+        nc.gpsimd.memset(key_scales[:].bitcast(I32), 0)
 
+        key_words = sb.tile([P, T], U16, align_bytes=64)
+        nc.sync.dma_start(key_words[:].bitcast(I32), keys_words[0].bitcast(I32))
         list2 = sb.tile([P, J // 16], U16)
         nc.sync.dma_start(list2[:], offs2)
         for quad in range(4):
@@ -50,18 +53,22 @@ def tile_attend_mixedslots_leaning_pagesums_kernel(
                 key_scales[32 * quad : 32 * quad + 4, :].bitcast(I32),
                 keys_scales[0, 4 * quad : 4 * quad + 4, :].bitcast(I32),
             )
-        key_words = sb.tile([P, T], U16, align_bytes=64)
-        nc.sync.dma_start(key_words[:].bitcast(I32), keys_words[0].bitcast(I32))
-        query_raw = sb.tile([P, PACK, Q], F32)
+        query_raw = sb.tile([P, PACK, Q], F32, align_bytes=64, tag="query_raw")
         nc.sync.dma_start(query_raw[:], query.rearrange("(p t) q -> p t q", t=PACK))
         mixer_rows = mixer.rearrange("(p t) i -> p t i", t=PACK)
-        mixer_raw = [sb.tile([P, PACK, HALF], F32, name=f"mixer_raw{h}") for h in range(2)]
-        nc.sync.dma_start(mixer_raw[0][:], mixer_rows[:, :, 0:HALF])
+        mixer_raw = [
+            sb.tile([P, PACK, hi - lo], F32, name=f"mixer_raw{c}", tag=f"mixer_raw{c}") for c, (lo, hi) in enumerate(CHUNKS)
+        ]
+        nc.sync.dma_start(mixer_raw[0][:], mixer_rows[:, :, slice(*CHUNKS[0])])
         list1 = sb.tile([P, I // 16], U16)
         nc.sync.dma_start(list1[:], offs)
-        nc.sync.dma_start(mixer_raw[1][:], mixer_rows[:, :, HALF:I])
+        nc.sync.dma_start(mixer_raw[1][:], mixer_rows[:, :, slice(*CHUNKS[1])])
+        hf_sb = sb.tile([P, PACK], F32, tag="hf")
+        nc.sync.dma_start(hf_sb[:], hf.rearrange("(p t) o -> p (t o)", t=PACK))
         worth_all = sb.tile([P, T], F32)
         nc.sync.dma_start(worth_all[:], worth)
+        lean_sb = sb.tile([P, 1], F32, tag="lean")
+        nc.sync.dma_start(lean_sb[:], lean)
         old_sb = sb.tile([P, M], F32)
         nc.sync.dma_start(old_sb[:], old)
         list3 = sb.tile([P, G // 16], U16)
@@ -69,22 +76,18 @@ def tile_attend_mixedslots_leaning_pagesums_kernel(
 
         identity = sb.tile([P, P], F32)
         make_identity(nc, identity[:])
-        hf_sb = sb.tile([P, PACK], F32)
-        nc.gpsimd.dma_start(hf_sb[:], hf.rearrange("(p t) o -> p (t o)", t=PACK))
-        lean_sb = sb.tile([P, 1], F32)
-        nc.gpsimd.dma_start(lean_sb[:], lean)
         placed = sb.tile([P, M], F32)
         nc.vector.memset(placed[:], 0.0)
-        lean_neg = sb.tile([P, 1], F32)
-        nc.gpsimd.tensor_scalar(lean_neg[:], lean_sb[:], -GAIN, 0.0, ALU.mult, ALU.add)
+        minus_one = sb.tile([P, 1], F32, tag="minus_one")
+        nc.vector.memset(minus_one[:], -1.0)
 
         warm = sb.tile([P, 1], F32)
         nc.scalar.activation(warm[:], placed[:, 0:1], ACT.Exp)
 
-        scales2 = sb.tile([P, J], U8, align_bytes=64)
-        nc.vector.tensor_copy(scales2[:], key_scales[:].indirect(list2[:]))
         words2 = sb.tile([P, J], U16, align_bytes=64)
         nc.vector.tensor_copy(words2[:], key_words[:].indirect(list2[:]))
+        scales2_lo = sb.tile([P, HALF], U8, align_bytes=64)
+        nc.vector.tensor_copy(scales2_lo[:], key_scales[:].indirect(list2[:, 0 : HALF // 16]))
 
         query_bf = sb.tile([P, Q, PACK], BF16, align_bytes=64)
         interleave(nc, query_bf[:], query_raw[:])
@@ -94,11 +97,15 @@ def tile_attend_mixedslots_leaning_pagesums_kernel(
             out=query_codes[:].bitcast(FP8X4), scales=query_scales[:], in_=query_bf[:].rearrange("p q t -> p (q t)")
         )
 
-        a0_ps = ps.tile([P, J], F32)
-        nc.tensor.matmul_mx(
-            out=a0_ps[:], lhsT=query_codes[:].bitcast(FP8X4), lhsT_scale=query_scales[:],
-            rhs=words2[:].bitcast(FP4X4), rhs_scale=scales2[:], start=True, stop=True,
-        )
+        a0_ps = ps.tile([P, J], F32, tag="scores")
+        scales2_hi = sb.tile([P, HALF], U8, align_bytes=64, tag="query_raw")
+        nc.vector.tensor_copy(scales2_hi[:], key_scales[:].indirect(list2[:, HALF // 16 : J // 16]))
+        for h, scales2 in enumerate((scales2_lo, scales2_hi)):
+            cols = slice(h * HALF, (h + 1) * HALF)
+            nc.tensor.matmul_mx(
+                out=a0_ps[:, cols], lhsT=query_codes[:].bitcast(FP8X4), lhsT_scale=query_scales[:],
+                rhs=words2[:, cols].bitcast(FP4X4), rhs_scale=scales2[:], start=True, stop=True,
+            )
 
         scales1 = sb.tile([P, I], U8, align_bytes=64)
         nc.vector.tensor_copy(scales1[:], key_scales[:].indirect(list1[:]))
@@ -107,7 +114,9 @@ def tile_attend_mixedslots_leaning_pagesums_kernel(
 
         mixer_codes = sb.tile([P, I], U32, align_bytes=64)
         mixer_scales = sb.tile([P, I], U8, align_bytes=64)
-        mixer_bf = [sb.tile([P, HALF, PACK], BF16, align_bytes=64, name=f"mixer_bf{h}") for h in range(2)]
+        mixer_bf = [
+            sb.tile([P, hi - lo, PACK], BF16, align_bytes=64, name=f"mixer_bf{c}") for c, (lo, hi) in enumerate(CHUNKS)
+        ]
         interleave(nc, mixer_bf[0][:], mixer_raw[0][:])
 
         a0_sb = sb.tile([P, PACK, P], F32)
@@ -118,7 +127,7 @@ def tile_attend_mixedslots_leaning_pagesums_kernel(
 
         interleave(nc, mixer_bf[1][:], mixer_raw[1][:])
 
-        s_ps = ps.tile([P, I], F32)
+        s_ps = ps.tile([P, I], F32, tag="scores")
         nc.tensor.matmul_mx(
             out=s_ps[:], lhsT=query_codes[:].bitcast(FP8X4), lhsT_scale=query_scales[:],
             rhs=words1[:].bitcast(FP4X4), rhs_scale=scales1[:], start=True, stop=False,
@@ -129,11 +138,11 @@ def tile_attend_mixedslots_leaning_pagesums_kernel(
             af_bf[:], a0t_ps[:].rearrange("p t q -> p q t"),
             hf_sb[:].unsqueeze(1).to_broadcast([P, Q, PACK]), ALU.mult,
         )
-        for h in range(2):
-            cols = slice(h * HALF, (h + 1) * HALF)
+        for c, chunk in enumerate(CHUNKS):
+            cols = slice(*chunk)
             nc.vector.quantize_mx(
                 out=mixer_codes[:, cols].bitcast(FP8X4), scales=mixer_scales[:, cols],
-                in_=mixer_bf[h][:].rearrange("p i t -> p (i t)"),
+                in_=mixer_bf[c][:].rearrange("p i t -> p (i t)"),
             )
         af_codes = sb.tile([P, Q], U32, align_bytes=64)
         af_scales = sb.tile([P, Q], U8, align_bytes=64)
@@ -145,33 +154,41 @@ def tile_attend_mixedslots_leaning_pagesums_kernel(
             rhs=mixer_codes[:].bitcast(FP8X4), rhs_scale=mixer_scales[:], start=False, stop=True,
         )
 
-        worth_slot = sb.tile([P, I], F32)
-        nc.vector.tensor_copy(worth_slot[:, 0:HALF], worth_all[:].indirect(list1[:, 0 : HALF // 16]))
+        worth_lo = sb.tile([P, HALF], F32, tag="hf")
+        nc.vector.tensor_copy(worth_lo[:], worth_all[:].indirect(list1[:, 0 : HALF // 16]))
 
-        s_neg = sb.tile([P, I], F32)
+        lean_gain = sb.tile([P, 1], F32)
+        nc.scalar.mul(lean_gain[:], lean_sb[:], GAIN)
+        s_neg = sb.tile([P, I], F32, tag="lean")
         max_neg = sb.tile([P, 1], F32)
-        nc.vector.tensor_scalar(s_neg[:], s_ps[:], -1.0, None, ALU.mult, ALU.min, accum_out=max_neg[:])
+        nc.vector.tensor_scalar(s_neg[:], s_ps[:], minus_one[:], None, ALU.mult, ALU.min, accum_out=max_neg[:])
         p = sb.tile([P, I], F32)
         p_sum = sb.tile([P, 1], F32)
         nc.scalar.activation(p[:], s_ps[:], ACT.Exp, bias=max_neg[:], accum_out=p_sum[:])
+        tilt_bias = sb.tile([P, 1], F32)
+        nc.scalar.activation(tilt_bias[:], max_neg[:], ACT.Identity, scale=lean_gain[:], bias=GAIN)
         tilt = sb.tile([P, I], F32)
-        nc.vector.tensor_scalar(tilt[:], s_neg[:], max_neg[:], lean_neg[:], ALU.subtract, ALU.mult)
-        nc.vector.tensor_copy(worth_slot[:, HALF:I], worth_all[:].indirect(list1[:, HALF // 16 : I // 16]))
+        nc.scalar.activation(tilt[:], s_ps[:], ACT.Identity, scale=lean_gain[:], bias=tilt_bias[:])
+        worth_hi = sb.tile([P, HALF], F32, tag="minus_one")
+        nc.vector.tensor_copy(worth_hi[:], worth_all[:].indirect(list1[:, HALF // 16 : I // 16]))
 
         p_inv = sb.tile([P, 1], F32)
         nc.vector.reciprocal(p_inv[:], p_sum[:])
-        p_tilt = sb.tile([P, I], F32)
-        tilt_sum = sb.tile([P, 1], F32)
-        nc.vector.scalar_tensor_tensor(p_tilt[:], tilt[:], -GAIN, p[:], ALU.add, ALU.mult, accum_out=tilt_sum[:])
+        p_depth = sb.tile([P, I], F32)
+        depth_sum = sb.tile([P, 1], F32)
+        nc.vector.scalar_tensor_tensor(
+            p_depth[:], s_neg[:], max_neg[:], p[:], ALU.subtract, ALU.mult, accum_out=depth_sum[:]
+        )
         share = sb.tile([P, I], F32)
-        nc.vector.scalar_tensor_tensor(share[:], p[:], p_inv[:], worth_slot[:], ALU.mult, ALU.mult)
+        nc.vector.scalar_tensor_tensor(share[:, 0:HALF], p[:, 0:HALF], p_inv[:], worth_lo[:], ALU.mult, ALU.mult)
+        nc.vector.scalar_tensor_tensor(share[:, HALF:I], p[:, HALF:I], p_inv[:], worth_hi[:], ALU.mult, ALU.mult)
         centre = sb.tile([P, 1], F32)
-        nc.vector.tensor_scalar(centre[:], tilt_sum[:], p_inv[:], None, ALU.mult)
+        nc.vector.tensor_scalar(centre[:], depth_sum[:], p_inv[:], lean_gain[:], ALU.mult, ALU.mult)
         ws = sb.tile([P, I], F32)
         wp = sb.tile([P, G], F32)
         for h in range(2):
             cols = slice(h * HALF, (h + 1) * HALF)
-            nc.vector.scalar_tensor_tensor(ws[:, cols], tilt[:, cols], centre[:], share[:, cols], ALU.subtract, ALU.mult)
+            nc.vector.scalar_tensor_tensor(ws[:, cols], tilt[:, cols], centre[:], share[:, cols], ALU.add, ALU.mult)
         for h in range(2):
             cols = slice(h * HALF, (h + 1) * HALF)
             nc.vector.tensor_reduce(

from contextlib import ExitStack

import concourse.mybir as mybir
from concourse.masks import make_identity

F32 = mybir.dt.float32
BF16 = mybir.dt.bfloat16
I32 = mybir.dt.int32
U32 = mybir.dt.uint32
U16 = mybir.dt.uint16
U8 = mybir.dt.uint8
FP8X4 = mybir.dt.float8_e4m3fn_x4
FP4X4 = mybir.dt.float4_e2m1fn_x4
ALU = mybir.AluOpType
ACT = mybir.ActivationFunctionType
AXIS = mybir.AxisListType

P = 128
PACK = 4
D, T, I, Q, J, G, M = 512, 2048, 512, 128, 512, 64, 512
RUN = I // G
HALF = I // 2
GAIN = 256.0
CHUNKS = ((0, 256), (256, 512))

FLOPS = 3 * 2 * 512 * 128 * 512


def interleave(nc, dst, src):
    nc.scalar.copy(
        out=dst.rearrange("p (c i) t -> p c t i", i=4),
        in_=src.rearrange("p t (c i) -> p c t i", i=4),
    )


def tile_attend_mixedslots_leaning_pagesums_kernel(
    tc, query, keys_words, keys_scales, hf, mixer, lean, worth, old, offs, offs2, offs3, out
):
    nc = tc.nc
    with ExitStack() as ctx:
        sb = ctx.enter_context(tc.tile_pool(name="sb", bufs=1))
        ps = ctx.enter_context(tc.psum_pool(name="ps", bufs=1))

        key_scales = sb.tile([P, T], U8, align_bytes=64)
        nc.gpsimd.memset(key_scales[:].bitcast(I32), 0)

        key_words = sb.tile([P, T], U16, align_bytes=64)
        nc.sync.dma_start(key_words[:].bitcast(I32), keys_words[0].bitcast(I32))
        list2 = sb.tile([P, J // 16], U16)
        nc.sync.dma_start(list2[:], offs2)
        for quad in range(4):
            nc.sync.dma_start(
                key_scales[32 * quad : 32 * quad + 4, :].bitcast(I32),
                keys_scales[0, 4 * quad : 4 * quad + 4, :].bitcast(I32),
            )
        query_raw = sb.tile([P, PACK, Q], F32, align_bytes=64, tag="query_raw")
        nc.sync.dma_start(query_raw[:], query.rearrange("(p t) q -> p t q", t=PACK))
        mixer_rows = mixer.rearrange("(p t) i -> p t i", t=PACK)
        mixer_raw = [
            sb.tile([P, PACK, hi - lo], F32, name=f"mixer_raw{c}", tag=f"mixer_raw{c}") for c, (lo, hi) in enumerate(CHUNKS)
        ]
        nc.sync.dma_start(mixer_raw[0][:], mixer_rows[:, :, slice(*CHUNKS[0])])
        list1 = sb.tile([P, I // 16], U16)
        nc.sync.dma_start(list1[:], offs)
        nc.sync.dma_start(mixer_raw[1][:], mixer_rows[:, :, slice(*CHUNKS[1])])
        hf_sb = sb.tile([P, PACK], F32, tag="hf")
        nc.sync.dma_start(hf_sb[:], hf.rearrange("(p t) o -> p (t o)", t=PACK))
        worth_all = sb.tile([P, T], F32)
        nc.sync.dma_start(worth_all[:], worth)
        lean_sb = sb.tile([P, 1], F32, tag="lean")
        nc.sync.dma_start(lean_sb[:], lean)
        old_sb = sb.tile([P, M], F32)
        nc.sync.dma_start(old_sb[:], old)
        list3 = sb.tile([P, G // 16], U16)
        nc.sync.dma_start(list3[:], offs3)

        identity = sb.tile([P, P], F32)
        make_identity(nc, identity[:])
        placed = sb.tile([P, M], F32)
        nc.vector.memset(placed[:], 0.0)
        minus_one = sb.tile([P, 1], F32, tag="minus_one")
        nc.vector.memset(minus_one[:], -1.0)

        warm = sb.tile([P, 1], F32)
        nc.scalar.activation(warm[:], placed[:, 0:1], ACT.Exp)

        words2 = sb.tile([P, J], U16, align_bytes=64)
        nc.vector.tensor_copy(words2[:], key_words[:].indirect(list2[:]))
        scales2_lo = sb.tile([P, HALF], U8, align_bytes=64)
        nc.vector.tensor_copy(scales2_lo[:], key_scales[:].indirect(list2[:, 0 : HALF // 16]))

        query_bf = sb.tile([P, Q, PACK], BF16, align_bytes=64)
        interleave(nc, query_bf[:], query_raw[:])
        query_codes = sb.tile([P, Q], U32, align_bytes=64)
        query_scales = sb.tile([P, Q], U8, align_bytes=64)
        nc.vector.quantize_mx(
            out=query_codes[:].bitcast(FP8X4), scales=query_scales[:], in_=query_bf[:].rearrange("p q t -> p (q t)")
        )

        a0_ps = ps.tile([P, J], F32, tag="scores")
        scales2_hi = sb.tile([P, HALF], U8, align_bytes=64, tag="query_raw")
        nc.vector.tensor_copy(scales2_hi[:], key_scales[:].indirect(list2[:, HALF // 16 : J // 16]))
        for h, scales2 in enumerate((scales2_lo, scales2_hi)):
            cols = slice(h * HALF, (h + 1) * HALF)
            nc.tensor.matmul_mx(
                out=a0_ps[:, cols], lhsT=query_codes[:].bitcast(FP8X4), lhsT_scale=query_scales[:],
                rhs=words2[:, cols].bitcast(FP4X4), rhs_scale=scales2[:], start=True, stop=True,
            )

        scales1 = sb.tile([P, I], U8, align_bytes=64)
        nc.vector.tensor_copy(scales1[:], key_scales[:].indirect(list1[:]))
        words1 = sb.tile([P, I], U16, align_bytes=64)
        nc.vector.tensor_copy(words1[:], key_words[:].indirect(list1[:]))

        mixer_codes = sb.tile([P, I], U32, align_bytes=64)
        mixer_scales = sb.tile([P, I], U8, align_bytes=64)
        mixer_bf = [
            sb.tile([P, hi - lo, PACK], BF16, align_bytes=64, name=f"mixer_bf{c}") for c, (lo, hi) in enumerate(CHUNKS)
        ]
        interleave(nc, mixer_bf[0][:], mixer_raw[0][:])

        a0_sb = sb.tile([P, PACK, P], F32)
        nc.scalar.copy(out=a0_sb[:], in_=a0_ps[:].rearrange("q (p t) -> q t p", t=PACK))
        a0t_ps = ps.tile([P, PACK, Q], F32)
        for t in range(PACK):
            nc.tensor.transpose(a0t_ps[:, t, :], a0_sb[:, t, :], identity[:])

        interleave(nc, mixer_bf[1][:], mixer_raw[1][:])

        s_ps = ps.tile([P, I], F32, tag="scores")
        nc.tensor.matmul_mx(
            out=s_ps[:], lhsT=query_codes[:].bitcast(FP8X4), lhsT_scale=query_scales[:],
            rhs=words1[:].bitcast(FP4X4), rhs_scale=scales1[:], start=True, stop=False,
        )

        af_bf = sb.tile([P, Q, PACK], BF16, align_bytes=64)
        nc.vector.tensor_tensor(
            af_bf[:], a0t_ps[:].rearrange("p t q -> p q t"),
            hf_sb[:].unsqueeze(1).to_broadcast([P, Q, PACK]), ALU.mult,
        )
        for c, chunk in enumerate(CHUNKS):
            cols = slice(*chunk)
            nc.vector.quantize_mx(
                out=mixer_codes[:, cols].bitcast(FP8X4), scales=mixer_scales[:, cols],
                in_=mixer_bf[c][:].rearrange("p i t -> p (i t)"),
            )
        af_codes = sb.tile([P, Q], U32, align_bytes=64)
        af_scales = sb.tile([P, Q], U8, align_bytes=64)
        nc.vector.quantize_mx(
            out=af_codes[:].bitcast(FP8X4), scales=af_scales[:], in_=af_bf[:].rearrange("p q t -> p (q t)")
        )
        nc.tensor.matmul_mx(
            out=s_ps[:], lhsT=af_codes[:].bitcast(FP8X4), lhsT_scale=af_scales[:],
            rhs=mixer_codes[:].bitcast(FP8X4), rhs_scale=mixer_scales[:], start=False, stop=True,
        )

        worth_lo = sb.tile([P, HALF], F32, tag="hf")
        nc.vector.tensor_copy(worth_lo[:], worth_all[:].indirect(list1[:, 0 : HALF // 16]))

        lean_gain = sb.tile([P, 1], F32)
        nc.scalar.mul(lean_gain[:], lean_sb[:], GAIN)
        s_neg = sb.tile([P, I], F32, tag="lean")
        max_neg = sb.tile([P, 1], F32)
        nc.vector.tensor_scalar(s_neg[:], s_ps[:], minus_one[:], None, ALU.mult, ALU.min, accum_out=max_neg[:])
        p = sb.tile([P, I], F32)
        p_sum = sb.tile([P, 1], F32)
        nc.scalar.activation(p[:], s_ps[:], ACT.Exp, bias=max_neg[:], accum_out=p_sum[:])
        tilt_bias = sb.tile([P, 1], F32)
        nc.scalar.activation(tilt_bias[:], max_neg[:], ACT.Identity, scale=lean_gain[:], bias=GAIN)
        tilt = sb.tile([P, I], F32)
        nc.scalar.activation(tilt[:], s_ps[:], ACT.Identity, scale=lean_gain[:], bias=tilt_bias[:])
        worth_hi = sb.tile([P, HALF], F32, tag="minus_one")
        nc.vector.tensor_copy(worth_hi[:], worth_all[:].indirect(list1[:, HALF // 16 : I // 16]))

        p_inv = sb.tile([P, 1], F32)
        nc.vector.reciprocal(p_inv[:], p_sum[:])
        p_depth = sb.tile([P, I], F32)
        depth_sum = sb.tile([P, 1], F32)
        nc.vector.scalar_tensor_tensor(
            p_depth[:], s_neg[:], max_neg[:], p[:], ALU.subtract, ALU.mult, accum_out=depth_sum[:]
        )
        share = sb.tile([P, I], F32)
        nc.vector.scalar_tensor_tensor(share[:, 0:HALF], p[:, 0:HALF], p_inv[:], worth_lo[:], ALU.mult, ALU.mult)
        nc.vector.scalar_tensor_tensor(share[:, HALF:I], p[:, HALF:I], p_inv[:], worth_hi[:], ALU.mult, ALU.mult)
        centre = sb.tile([P, 1], F32)
        nc.vector.tensor_scalar(centre[:], depth_sum[:], p_inv[:], lean_gain[:], ALU.mult, ALU.mult)
        ws = sb.tile([P, I], F32)
        wp = sb.tile([P, G], F32)
        for h in range(2):
            cols = slice(h * HALF, (h + 1) * HALF)
            nc.vector.scalar_tensor_tensor(ws[:, cols], tilt[:, cols], centre[:], share[:, cols], ALU.add, ALU.mult)
        for h in range(2):
            cols = slice(h * HALF, (h + 1) * HALF)
            nc.vector.tensor_reduce(
                wp[:, h * (G // 2) : (h + 1) * (G // 2)],
                ws[:, cols].rearrange("q (g r) -> q g r", r=RUN), AXIS.X, ALU.add,
            )
        nc.vector.tensor_copy(placed[:].indirect(list3[:]), wp[:])
        result = sb.tile([P, M], F32)
        for h, queue in enumerate((nc.sync, nc.scalar)):
            cols = slice(h * (M // 2), (h + 1) * (M // 2))
            nc.vector.tensor_tensor(result[:, cols], placed[:, cols], old_sb[:, cols], ALU.add)
            queue.dma_start(out[:, cols], result[:, cols])
